import numpy as np
import ml_dtypes


def mxq(x, axis, fmt="e4m3"):
    dtype, down = {"e4m3": (ml_dtypes.float8_e4m3fn, 7), "e5m2": (ml_dtypes.float8_e5m2, 14)}[fmt]
    v = np.moveaxis(np.asarray(x, np.float32).astype(ml_dtypes.bfloat16).astype(np.float64), axis, -1)
    blocks = v.reshape(v.shape[:-1] + (-1, 32))
    amax = np.abs(blocks).max(-1, keepdims=True)
    byte = np.maximum(np.where(amax > 0, np.frexp(amax)[1] - 1 + 127, 0) - down, 1)
    scale = np.exp2(byte - 127.0)
    codes = (blocks / scale).astype(np.float32).astype(dtype).astype(np.float64)
    return np.moveaxis((codes * scale).reshape(v.shape), -1, axis)


WIDE = False


def mx_kscale(k):
    if not WIDE:
        return np.ones(k)
    levels = np.array([10, -10, 5, -5, 0])
    if k % 512:
        return np.exp2(np.random.permutation(np.resize(levels, k // 32))).repeat(32)
    a = np.empty((k // 512, 16))
    for p in range(k // 512):
        a[p, :8] = np.random.permutation(np.resize(levels, 8))
        for g in range(8):
            far = levels[np.abs(levels - a[p, g]) >= 10]
            a[p, g + 8] = far[np.random.randint(len(far))]
    return np.exp2(a.ravel()).repeat(32)


def f64(x):
    return np.asarray(x).astype(np.float64)


def striped(idx):
    return np.tile(idx.reshape(-1, 16).T, (8, 1)).astype(np.uint16)


def unstriped(offs):
    return offs[:16].T.reshape(-1).astype(np.int64)


E2M1 = np.array([0.0, 0.5, 1.0, 1.5, 2.0, 3.0, 4.0, 6.0, -0.0, -0.5, -1.0, -1.5, -2.0, -3.0, -4.0, -6.0])


def pack_weight(w, fmt):
    k, n = w.shape
    w = f64(np.asarray(w, np.float32).astype(ml_dtypes.bfloat16)).reshape(k // 32, 32, n)
    amax = np.abs(w).max(1)
    if fmt == "e4m3":
        byte = np.frexp(amax)[1] - 1 + 127 - 7
    else:
        mant, ex = np.frexp(amax / 6.0)
        byte = np.where(mant > 0.5, ex, ex - 1) + 127
    byte = np.clip(np.where(amax > 0, byte, 1), 1, 254)
    scaled = (w * np.exp2(127.0 - byte)[:, None, :]).reshape(k, n).astype(np.float32)
    by_word = np.ascontiguousarray(scaled.reshape(k // 512, 128, 4, n).transpose(0, 1, 3, 2))
    if fmt == "e4m3":
        words = by_word.astype(ml_dtypes.float8_e4m3fn).view(np.uint8)
    else:
        c = by_word.astype(ml_dtypes.float4_e2m1fn).view(np.uint8) & 0xF
        words = (c[..., 0::2] | (c[..., 1::2] << 4)).reshape(k // 512, 128, 2 * n)
    return np.ascontiguousarray(words), np.ascontiguousarray(byte.astype(np.uint8).reshape(k // 512, 16, n))


def unpack_weight(words, scales, fmt):
    g, _, n = scales.shape
    words = np.ascontiguousarray(words).reshape(g, 128, n, -1)
    if fmt == "e4m3":
        vals = words.view(ml_dtypes.float8_e4m3fn).astype(np.float64)
    else:
        nib = np.empty((g, 128, n, 4), np.uint8)
        nib[..., 0::2] = words & 0xF
        nib[..., 1::2] = words >> 4
        vals = E2M1[nib]
    vals = vals * np.repeat(np.exp2(scales.astype(np.float64) - 127.0), 8, axis=1)[..., None]
    return vals.transpose(0, 1, 3, 2).reshape(g * 512, n)


def gelu(v):
    return 0.5 * v * (1.0 + np.tanh(np.sqrt(2.0 / np.pi) * (v + 0.044715 * v**3)))


def bf(x):
    return np.asarray(x, np.float32).astype(ml_dtypes.bfloat16)


def planes(Y):
    n, m = Y.shape
    b = f64(bf(Y)).reshape(n // 32, 32, m)
    amax = np.abs(b).max(1)
    byte = np.clip(np.where(amax > 0, np.frexp(amax)[1] - 1 + 127 - 7, 1), 1, 254)
    codes = (b * np.exp2(127.0 - byte)[:, None, :]).reshape(n, m).astype(np.float32).astype(ml_dtypes.float8_e4m3fn).view(np.uint8)
    words = codes.reshape(n // 512, 128, 4, m).transpose(0, 1, 3, 2)
    return np.ascontiguousarray(words), np.ascontiguousarray(byte.astype(np.uint8).reshape(n // 512, 16, m))


K, H, N, T, S, T2, P = 1024, 512, 1024, 4096, 1024, 2048, 1024

def setup_inputs():
    n = np.random.standard_normal
    sk = mx_kscale(K)[:, None]
    u = mx_kscale(H)[:, None]
    tab_words, tab_scales = pack_weight(n((K, T)) * sk, "e4m3")
    w2_words, w2_scales = pack_weight(0.95 * n((H, H)) / np.sqrt(H) / u, "e2m1")
    w4_words, w4_scales = pack_weight(n((H, N)) / np.sqrt(H) / u, "e4m3")
    sign = np.random.choice([-1.0, 1.0], H)
    return {
        "tab_words": tab_words, "tab_scales": tab_scales,
        "offs": striped(np.random.permutation(T)[:S]),
        "offs2": striped(np.random.permutation(T2)[:S]),
        "offs3": striped(np.random.permutation(T2)[:P]),
        "w1": (0.95 * n((K, H)) / np.sqrt(K) / sk).astype(np.float32),
        "w2_words": w2_words, "w2_scales": w2_scales,
        "w3": (0.6 * n((K, H)) / np.sqrt(K) / sk).astype(np.float32),
        "gain": (np.random.uniform(0.6, 2.0, H) * u[:, 0]).astype(np.float32),
        "page0": (0.8 * n((H, T2))).astype(np.float32),
        "wgs": np.exp(0.3 * n((128, S))).astype(np.float32),
        "steep": np.random.uniform(0.6, 3.0, H).astype(np.float32),
        "shift": n(H).astype(np.float32),
        "expect": (0.3 + 0.25 * n((H, P))).astype(np.float32),
        "lean": (sign * np.random.uniform(0.8, 2.5, H) * u[:, 0]).astype(np.float32),
        "w4_words": w4_words, "w4_scales": w4_scales,
        "size": np.exp(0.8 * n(N)).astype(np.float32),
    }

def reference(tab_words, tab_scales, offs, offs2, offs3, w1, w2_words, w2_scales, w3, gain, page0, wgs, steep, shift, expect, lean, w4_words, w4_scales, size):
    v = unpack_weight(tab_words, tab_scales, "e4m3")[:, unstriped(offs)]
    w2 = unpack_weight(w2_words, w2_scales, "e2m1")
    w4 = unpack_weight(w4_words, w4_scales, "e4m3")
    p = mxq(f64(w1), 0, "e4m3").T @ v
    q = mxq(f64(gain)[:, None] * (p / (1.0 + np.exp(-p))), 0, "e4m3")
    h = np.minimum(w2.T @ q + mxq(f64(w3), 0, "e4m3").T @ v, p)
    page = f64(page0).copy()
    page[:, unstriped(offs2)] = np.tile(f64(wgs), (H // 128, 1)) * h
    a = 1.0 / (1.0 + np.exp(-(f64(steep)[:, None] * page[:, unstriped(offs3)] + f64(shift)[:, None])))
    x = mxq(f64(lean)[:, None] * (a - f64(expect)), 0, "e4m3")
    y = f64(size)[:, None] * (w4.T @ x)
    words, scales = planes(y)
    return y, words, scales

@@ -1,0 +1,348 @@
+from contextlib import ExitStack
+
+import concourse.mybir as mybir
+
+K, H, N, T, S, T2, J = 1024, 512, 1024, 4096, 1024, 2048, 1024
+FLOPS = 2 * (2 * K * H * S + H * H * S + H * N * J)
+
+F32 = mybir.dt.float32
+BF16 = mybir.dt.bfloat16
+I32 = mybir.dt.int32
+U32 = mybir.dt.uint32
+U16 = mybir.dt.uint16
+U8 = mybir.dt.uint8
+FP8X4 = mybir.dt.float8_e4m3fn_x4
+FP4X4 = mybir.dt.float4_e2m1fn_x4
+ALU = mybir.AluOpType
+ACT = mybir.ActivationFunctionType
+
+P = 128
+PACK = 4
+HALF = 512
+BLK = 128
+LIST_COLS = HALF // 16
+
+
+def tile_list_lamp_wear_log_kernel(
+    tc, tab_words, tab_scales, offs, offs2, offs3, w1, w2_words, w2_scales, w3, gain, page0, wgs,
+    steep, shift, expect, lean, w4_words, w4_scales, size, out_0, out_1, out_2,
+):
+    nc = tc.nc
+    with ExitStack() as ctx:
+        lists = ctx.enter_context(tc.tile_pool(name="lists", bufs=1))
+        keep = ctx.enter_context(tc.tile_pool(name="keep", bufs=1))
+        ring = ctx.enter_context(tc.tile_pool(name="ring", bufs=2))
+        psum = ctx.enter_context(tc.psum_pool(name="psum", bufs=4))
+
+        def held(shape, dtype, name):
+            return keep.tile(shape, dtype, name=name, align_bytes=64)
+
+        def turn(shape, dtype, name, tag, bufs):
+            return ring.tile(shape, dtype, name=name, tag=tag, bufs=bufs, align_bytes=64)
+
+        idx1 = lists.tile([P, S // 16], U16, name="idx1")
+        idx2 = lists.tile([P, S // 16], U16, name="idx2")
+        idx3 = lists.tile([P, J // 16], U16, name="idx3")
+
+        tab_sc = held([P, T], U8, "tab_sc")
+        w2_sc_raw = held([P, H], U8, "w2_sc_raw")
+        w4_sc_raw = held([P, N], U8, "w4_sc_raw")
+
+        def load_table(a):
+            words = turn([P, T], I32, "tab%d" % a, "wide", 2)
+            nc.sync.dma_start(out=words[:], in_=tab_words[a].rearrange("p t i -> p (t i)").bitcast(I32))
+            return words
+
+        def load_weight(w, a, name):
+            raw = turn([P, PACK, H], F32, name, "stage", 4)
+            nc.sync.dma_start(out=raw[:], in_=w[512 * a : 512 * (a + 1), :].rearrange("(p j) c -> p j c", j=PACK))
+            return raw
+
+        wgs_rows = wgs.rearrange("(p t) j -> p t j", t=PACK)
+
+        def load_wgs(t0, t1, half, name):
+            dealt = held([P, t1 - t0, HALF], F32, name)
+            for quad in (0, 2, 1, 3):
+                nc.sync.dma_start(
+                    out=dealt[32 * quad : 32 * quad + 32],
+                    in_=wgs_rows[:, t0:t1, HALF * half : HALF * (half + 1)],
+                )
+            return dealt
+
+        page_rows = page0.rearrange("(p t) c -> p t c", t=PACK)
+
+        def load_page(t):
+            page = held([P, T2], F32, "page%d" % t)
+            nc.sync.dma_start(out=page[:], in_=page_rows[:, t, :])
+            return page
+
+        def load_row_values(vec, name):
+            col = held([P, PACK], F32, name)
+            nc.sync.dma_start(out=col[:], in_=vec.rearrange("(p t) -> p t", t=PACK))
+            return col
+
+        def load_scale_rows(plane, rows):
+            nc.gpsimd.memset(plane[:].bitcast(I32), 0)
+            for quad in range(4):
+                nc.gpsimd.dma_start(
+                    out=plane[32 * quad : 32 * quad + 4, :].bitcast(I32),
+                    in_=rows[0, 4 * quad : 4 * quad + 4, :].bitcast(I32),
+                )
+
+        nc.vector.memset(tab_sc[:].bitcast(I32), 0)
+        tab = [load_table(0)]
+        for quad in range(4):
+            nc.sync.dma_start(
+                out=tab_sc[32 * quad : 32 * quad + 8, :].bitcast(I32),
+                in_=tab_scales[:, 4 * quad : 4 * quad + 4, :].bitcast(I32),
+            )
+        nc.sync.dma_start(idx1[:], offs)
+        w1_raw = [load_weight(w1, 0, "w1raw0")]
+        w2_raw = held([P, 2 * H], U8, "w2_raw")
+        nc.sync.dma_start(out=w2_raw[:].bitcast(I32), in_=w2_words[0].bitcast(I32))
+        tab.append(load_table(1))
+        w1_raw.append(load_weight(w1, 1, "w1raw1"))
+        gain_c = load_row_values(gain, "gain_c")
+        w3_raw = [load_weight(w3, 0, "w3raw0"), load_weight(w3, 1, "w3raw1")]
+        wg_first = load_wgs(0, 1, 0, "wg_first")
+        nc.sync.dma_start(idx2[:], offs2)
+        pages = [load_page(0)]
+        wg_rest = load_wgs(1, PACK, 0, "wg_rest")
+        for t in range(1, PACK):
+            pages.append(load_page(t))
+        nc.sync.dma_start(idx3[:], offs3)
+        wg_late = load_wgs(0, PACK, 1, "wg_late")
+
+        steep_c = load_row_values(steep, "steep_c")
+        shift_c = load_row_values(shift, "shift_c")
+        lean_c = load_row_values(lean, "lean_c")
+        size_c = held([P, 2, PACK], F32, "size_c")
+        nc.sync.dma_start(out=size_c[:], in_=size.rearrange("(g p t) -> p g t", g=2, t=PACK))
+
+        def wg(t, half):
+            if half == 1:
+                return wg_late[:, t, :]
+            return wg_first[:, 0, :] if t == 0 else wg_rest[:, t - 1, :]
+
+        load_scale_rows(w2_sc_raw, w2_scales)
+        load_scale_rows(w4_sc_raw, w4_scales)
+        w2_sc = held([P, H], U8, "w2_sc")
+        nc.gpsimd.tensor_copy(
+            out=w2_sc[:].rearrange("p (t m) -> p t m", t=PACK),
+            in_=w2_sc_raw[:].rearrange("p (m t) -> p t m", t=PACK),
+        )
+        w4_sc = held([P, N], U8, "w4_sc")
+        nc.gpsimd.tensor_copy(
+            out=w4_sc[:].rearrange("p (g t m) -> p g t m", g=2, t=PACK),
+            in_=w4_sc_raw[:].rearrange("p (g m t) -> p g t m", g=2, t=PACK),
+        )
+
+        def gather_words(a, half):
+            got = held([P, HALF], U32, "v%d_%d" % (a, half))
+            nc.vector.tensor_copy(
+                got[:], tab[a][:].bitcast(U32).indirect(idx1[:, LIST_COLS * half : LIST_COLS * (half + 1)])
+            )
+            return got
+
+        def gather_scales(half):
+            got = held([P, HALF], U8, "vs%d" % half)
+            nc.vector.tensor_copy(got[:], tab_sc[:].indirect(idx1[:, LIST_COLS * half : LIST_COLS * (half + 1)]))
+            return got
+
+        def round_weight(raw, pair, engine, name):
+            grouped = turn([P, 2 * BLK * PACK], BF16, name, "wbf", 4)
+            dst = grouped[:].rearrange("p (t m j) -> p m t j", t=2, j=PACK)
+            src = raw[:].rearrange("p j (m t) -> p m t j", t=PACK)[:, :, 2 * pair : 2 * pair + 2, :]
+            if engine == "vector":
+                nc.vector.tensor_copy(out=dst, in_=src)
+            else:
+                nc.scalar.copy(out=dst, in_=src)
+            return grouped
+
+        def quantize(grouped, codes, scales):
+            nc.vector.quantize_mx(out=codes.bitcast(FP8X4), scales=scales, in_=grouped)
+
+        def quantize_weight(grouped, name):
+            codes = held([P, 2 * BLK], U32, name + "c")
+            scales = held([P, 2 * BLK], U8, name + "s")
+            quantize(grouped[:], codes[:], scales[:])
+            return codes, scales
+
+        def stationary(pieces, t):
+            codes, scales = pieces[t // 2]
+            cols = slice(BLK * (t % 2), BLK * (t % 2 + 1))
+            return codes[:, cols].bitcast(FP8X4), scales[:, cols]
+
+        v = {}
+        v[0, 0] = gather_words(0, 0)
+        vs = [gather_scales(0)]
+        w1a_g = [round_weight(w1_raw[0], pair, "scalar", "w1a%d" % pair) for pair in range(2)]
+        w1q = [[quantize_weight(w1a_g[pair], "w1a%d" % pair) for pair in range(2)]]
+        w2_dealt = held([P, 2 * H], U8, "w2_dealt")
+        nc.scalar.copy(
+            out=w2_dealt[:].bitcast(U16).rearrange("p (t m) -> p t m", t=PACK),
+            in_=w2_raw[:].bitcast(U16).rearrange("p (m t) -> p t m", t=PACK),
+        )
+        v[0, 1] = gather_words(0, 1)
+        vs.append(gather_scales(1))
+
+        def p_pass(bank, a, half, b):
+            cols = slice(BLK * b, BLK * (b + 1))
+            for t in range(PACK):
+                lhs, lhs_sc = stationary(w1q[a], t)
+                nc.tensor.matmul_mx(
+                    out=bank[:, BLK * t : BLK * (t + 1)], lhsT=lhs, lhsT_scale=lhs_sc,
+                    rhs=v[a, half][:, cols].bitcast(FP8X4), rhs_scale=vs[half][4 * a :, cols],
+                    start=(a == 0 and t == 0), stop=(a == 1 and t == PACK - 1),
+                )
+
+        p_banks = [psum.tile([P, HALF], F32, name="p0_%d" % b, tag="pb") for b in range(4)]
+        for b in range(4):
+            p_pass(p_banks[b], 0, 0, b)
+
+        v[1, 0] = gather_words(1, 0)
+        w1b_g = [round_weight(w1_raw[1], 0, "vector", "w1b0"), round_weight(w1_raw[1], 1, "scalar", "w1b1")]
+        w1q.append([quantize_weight(w1b_g[pair], "w1b%d" % pair) for pair in range(2)])
+        v[1, 1] = gather_words(1, 1)
+
+        gain_b = gain_c[:].unsqueeze(1).to_broadcast([P, BLK, PACK])
+
+        def make_q(banks, half):
+            q_codes = held([P, HALF], U32, "qc%d" % half)
+            q_scales = held([P, HALF], U8, "qs%d" % half)
+            p_kept = turn([P, PACK, HALF], F32, "p_kept%d" % half, "kept", 2)
+            rounded = []
+            for b in range(4):
+                silu = turn([P, BLK, PACK], F32, "silu%d_%d" % (half, b), "silu", 3)
+                nc.scalar.activation(out=silu[:], in_=banks[b][:].rearrange("p (t n) -> p n t", t=PACK), func=ACT.Silu)
+                q_bf = turn([P, BLK, PACK], BF16, "qbf%d_%d" % (half, b), "qbf", 4)
+                nc.vector.tensor_tensor(out=q_bf[:], in0=silu[:], in1=gain_b, op=ALU.mult)
+                rounded.append(q_bf)
+            for b in range(4):
+                cols = slice(BLK * b, BLK * (b + 1))
+                quantize(rounded[b][:].rearrange("p n t -> p (n t)"), q_codes[:, cols], q_scales[:, cols])
+            for b in range(4):
+                nc.scalar.copy(
+                    out=p_kept[:, :, BLK * b : BLK * (b + 1)], in_=banks[b][:].rearrange("p (t n) -> p t n", t=PACK)
+                )
+            return q_codes, q_scales, p_kept
+
+        for b in range(4):
+            p_pass(p_banks[b], 1, 0, b)
+        stage1 = [make_q(p_banks, 0)]
+
+        w3q = [[None, None], [None, None]]
+        for a in range(2):
+            w3q[a][0] = quantize_weight(round_weight(w3_raw[a], 0, "vector", "w3%d0" % a), "w3%d0" % a)
+
+        def refresh(t, half):
+            q_codes, q_scales, p_kept = stage1[half]
+            bank = psum.tile([P, HALF], F32, name="s%d_%d" % (t, half), tag="sb")
+            lhs, lhs_sc = stationary(w3q[0], t)
+            nc.tensor.matmul_mx(
+                out=bank[:], lhsT=lhs, lhsT_scale=lhs_sc, rhs=v[0, half][:].bitcast(FP8X4), rhs_scale=vs[half][:],
+                start=True, stop=False,
+            )
+            nc.tensor.matmul_mx(
+                out=bank[:], lhsT=w2_dealt[:, 2 * BLK * t : 2 * BLK * (t + 1)].bitcast(FP4X4),
+                lhsT_scale=w2_sc[:, BLK * t : BLK * (t + 1)], rhs=q_codes[:].bitcast(FP8X4), rhs_scale=q_scales[:],
+                start=False, stop=False,
+            )
+            lhs, lhs_sc = stationary(w3q[1], t)
+            nc.tensor.matmul_mx(
+                out=bank[:], lhsT=lhs, lhsT_scale=lhs_sc, rhs=v[1, half][:].bitcast(FP8X4), rhs_scale=vs[half][4:, :],
+                start=False, stop=True,
+            )
+            h = turn([P, HALF], F32, "h%d_%d" % (t, half), "h", 3)
+            nc.vector.tensor_tensor(out=h[:], in0=bank[:], in1=p_kept[:, t, :], op=ALU.min)
+            nc.vector.tensor_tensor(
+                pages[t][:].indirect(idx2[:, LIST_COLS * half : LIST_COLS * (half + 1)]), h[:], wg(t, half), ALU.mult
+            )
+
+        refresh(0, 0)
+        for a in range(2):
+            w3q[a][1] = quantize_weight(round_weight(w3_raw[a], 1, "scalar", "w3%d1" % a), "w3%d1" % a)
+        refresh(1, 0)
+        p_banks = [psum.tile([P, HALF], F32, name="p1_%d" % b, tag="pb") for b in range(4)]
+        for b in range(4):
+            for a in range(2):
+                p_pass(p_banks[b], a, 1, b)
+        refresh(2, 0)
+        refresh(3, 0)
+        stage1.append(make_q(p_banks, 1))
+
+        w4_raw = held([P, N], I32, "w4_raw")
+        nc.sync.dma_start(out=w4_raw[:], in_=w4_words[0].rearrange("p c i -> p (c i)").bitcast(I32))
+        expected = turn([P, PACK, J], F32, "expected", "wide", 2)
+        nc.sync.dma_start(out=expected[:], in_=expect.rearrange("(p t) j -> p t j", t=PACK))
+        leaned = turn([P, PACK, J], F32, "leaned", "wide", 2)
+
+        for t in range(PACK):
+            refresh(t, 1)
+
+        def look(t, half):
+            nc.scalar.activation(
+                out=gate[:, t, HALF * half : HALF * (half + 1)],
+                in_=pages[t][:].indirect(idx3[:, LIST_COLS * half : LIST_COLS * (half + 1)]),
+                func=ACT.Sigmoid, bias=shift_c[:, t : t + 1], scale=steep_c[:, t : t + 1],
+            )
+
+        for t in range(PACK):
+            nc.scalar.activation(out=leaned[:, t, :], in_=expected[:, t, :], func=ACT.Copy, scale=lean_c[:, t : t + 1])
+        w4_dealt = held([P, N], U32, "w4_dealt")
+        nc.scalar.copy(
+            out=w4_dealt[:].rearrange("p (g t m) -> p g t m", g=2, t=PACK),
+            in_=w4_raw[:].bitcast(U32).rearrange("p (g m t) -> p g t m", g=2, t=PACK),
+        )
+        gate = turn([P, PACK, J], F32, "gate", "wide", 2)
+        for t in range(PACK):
+            for half in range(2):
+                look(t, half)
+
+        y = {}
+        for half in range(2):
+            cols = slice(HALF * half, HALF * (half + 1))
+            x_rows = turn([P, PACK, HALF], BF16, "x_rows%d" % half, "x_rows", 1)
+            for t in range(PACK):
+                nc.vector.scalar_tensor_tensor(
+                    out=x_rows[:, t, :], in0=gate[:, t, cols], scalar=lean_c[:, t : t + 1], in1=leaned[:, t, cols],
+                    op0=ALU.mult, op1=ALU.subtract,
+                )
+            x_bf = held([P, HALF, PACK], BF16, "x_bf%d" % half)
+            nc.vector.tensor_copy(out=x_bf[:], in_=x_rows[:].rearrange("p t j -> p j t"))
+            x_codes = held([P, HALF], U32, "xc%d" % half)
+            x_scales = held([P, HALF], U8, "xs%d" % half)
+            quantize(x_bf[:].rearrange("p j t -> p (j t)"), x_codes[:], x_scales[:])
+            for g in range(2):
+                y[g, half] = turn([P, PACK, HALF], F32, "y%d_%d" % (g, half), "stage", 4)
+                rows = out_0[512 * g : 512 * (g + 1), cols].rearrange("(p t) j -> p t j", t=PACK)
+                for t in range(PACK):
+                    wcols = slice(512 * g + BLK * t, 512 * g + BLK * (t + 1))
+                    bank = psum.tile([P, HALF], F32, name="y%d_%d_%d" % (g, half, t), tag=("pb", "sb")[g])
+                    nc.tensor.matmul_mx(
+                        out=bank[:], lhsT=w4_dealt[:, wcols].bitcast(FP8X4), lhsT_scale=w4_sc[:, wcols],
+                        rhs=x_codes[:].bitcast(FP8X4), rhs_scale=x_scales[:], start=True, stop=True,
+                    )
+                    nc.scalar.activation(
+                        out=y[g, half][:, t, :], in_=bank[:], func=ACT.Copy, scale=size_c[:, g, t : t + 1]
+                    )
+                    if t % 2 == 1:
+                        nc.sync.dma_start(out=rows[:, t - 1 : t + 1, :], in_=y[g, half][:, t - 1 : t + 1, :])
+
+        y_scales = held([P, 2, J], U8, "y_scales")
+        for half in range(2):
+            cols = slice(HALF * half, HALF * (half + 1))
+            for g in range(2):
+                y_bf = turn([P, HALF, PACK], BF16, "y_bf%d_%d" % (g, half), "kept", 2)
+                nc.vector.tensor_copy(out=y_bf[:], in_=y[g, half][:].rearrange("p t j -> p j t"))
+                y_codes = held([P, HALF], U32, "yc%d_%d" % (g, half))
+                quantize(y_bf[:].rearrange("p j t -> p (j t)"), y_codes[:], y_scales[:, g, cols])
+                nc.sync.dma_start(
+                    out=out_1[g].rearrange("p m t -> p (m t)").bitcast(I32)[:, cols], in_=y_codes[:].bitcast(I32)
+                )
+        for quad in range(4):
+            queue = nc.sync if quad % 2 == 0 else nc.scalar
+            queue.dma_start(
+                out=out_2[:, 4 * quad : 4 * quad + 4, :].rearrange("g r m -> r g m").bitcast(I32),
+                in_=y_scales[32 * quad : 32 * quad + 4].bitcast(I32),
+            )

@@ -19,6 +19,7 @@ ACT = mybir.ActivationFunctionType
 P = 128
 PACK = 4
 HALF = 512
+QUARTER = 256
 BLK = 128
 LIST_COLS = HALF // 16
 
@@ -81,15 +82,16 @@ def tile_list_lamp_wear_log_kernel(
             nc.sync.dma_start(out=col[:], in_=vec.rearrange("(p t) -> p t", t=PACK))
             return col
 
-        def load_scale_rows(plane, rows):
-            nc.gpsimd.memset(plane[:].bitcast(I32), 0)
+        def load_scale_rows(plane, rows, queue):
             for quad in range(4):
-                nc.gpsimd.dma_start(
+                queue.dma_start(
                     out=plane[32 * quad : 32 * quad + 4, :].bitcast(I32),
                     in_=rows[0, 4 * quad : 4 * quad + 4, :].bitcast(I32),
                 )
 
         nc.vector.memset(tab_sc[:].bitcast(I32), 0)
+        nc.gpsimd.memset(w2_sc_raw[:].bitcast(I32), 0)
+        nc.gpsimd.memset(w4_sc_raw[:].bitcast(I32), 0)
         tab = [load_table(0)]
         for quad in range(4):
             nc.sync.dma_start(
@@ -100,8 +102,9 @@ def tile_list_lamp_wear_log_kernel(
         w1_raw = [load_weight(w1, 0, "w1raw0")]
         w2_raw = held([P, 2 * H], U8, "w2_raw")
         nc.sync.dma_start(out=w2_raw[:].bitcast(I32), in_=w2_words[0].bitcast(I32))
-        tab.append(load_table(1))
+        load_scale_rows(w2_sc_raw, w2_scales, nc.sync)
         w1_raw.append(load_weight(w1, 1, "w1raw1"))
+        tab.append(load_table(1))
         gain_c = load_row_values(gain, "gain_c")
         w3_raw = [load_weight(w3, 0, "w3raw0"), load_weight(w3, 1, "w3raw1")]
         wg_first = load_wgs(0, 1, 0, "wg_first")
@@ -124,13 +127,7 @@ def tile_list_lamp_wear_log_kernel(
                 return wg_late[:, t, :]
             return wg_first[:, 0, :] if t == 0 else wg_rest[:, t - 1, :]
 
-        load_scale_rows(w2_sc_raw, w2_scales)
-        load_scale_rows(w4_sc_raw, w4_scales)
-        w2_sc = held([P, H], U8, "w2_sc")
-        nc.gpsimd.tensor_copy(
-            out=w2_sc[:].rearrange("p (t m) -> p t m", t=PACK),
-            in_=w2_sc_raw[:].rearrange("p (m t) -> p t m", t=PACK),
-        )
+        load_scale_rows(w4_sc_raw, w4_scales, nc.gpsimd)
         w4_sc = held([P, N], U8, "w4_sc")
         nc.gpsimd.tensor_copy(
             out=w4_sc[:].rearrange("p (g t m) -> p g t m", g=2, t=PACK),
@@ -149,8 +146,8 @@ def tile_list_lamp_wear_log_kernel(
             nc.vector.tensor_copy(got[:], tab_sc[:].indirect(idx1[:, LIST_COLS * half : LIST_COLS * (half + 1)]))
             return got
 
-        def round_weight(raw, pair, engine, name):
-            grouped = turn([P, 2 * BLK * PACK], BF16, name, "wbf", 4)
+        def round_weight(raw, pair, engine, name, tag="wbf"):
+            grouped = turn([P, 2 * BLK * PACK], BF16, name, tag, 3)
             dst = grouped[:].rearrange("p (t m j) -> p m t j", t=2, j=PACK)
             src = raw[:].rearrange("p j (m t) -> p m t j", t=PACK)[:, :, 2 * pair : 2 * pair + 2, :]
             if engine == "vector":
@@ -185,6 +182,11 @@ def tile_list_lamp_wear_log_kernel(
         )
         v[0, 1] = gather_words(0, 1)
         vs.append(gather_scales(1))
+        w2_sc = held([P, H], U8, "w2_sc")
+        nc.vector.tensor_copy(
+            out=w2_sc[:].rearrange("p (t m) -> p t m", t=PACK),
+            in_=w2_sc_raw[:].rearrange("p (m t) -> p t m", t=PACK),
+        )
 
         def p_pass(bank, a, half, b):
             cols = slice(BLK * b, BLK * (b + 1))
@@ -200,9 +202,9 @@ def tile_list_lamp_wear_log_kernel(
         for b in range(4):
             p_pass(p_banks[b], 0, 0, b)
 
-        v[1, 0] = gather_words(1, 0)
         w1b_g = [round_weight(w1_raw[1], 0, "vector", "w1b0"), round_weight(w1_raw[1], 1, "scalar", "w1b1")]
         w1q.append([quantize_weight(w1b_g[pair], "w1b%d" % pair) for pair in range(2)])
+        v[1, 0] = gather_words(1, 0)
         v[1, 1] = gather_words(1, 1)
 
         gain_b = gain_c[:].unsqueeze(1).to_broadcast([P, BLK, PACK])
@@ -227,6 +229,31 @@ def tile_list_lamp_wear_log_kernel(
                 )
             return q_codes, q_scales, p_kept
 
+        def make_q_on_scalar(half):
+            q_codes = held([P, HALF], U32, "qc%d" % half)
+            q_scales = held([P, HALF], U8, "qs%d" % half)
+            p_kept = turn([P, PACK, HALF], F32, "p_kept%d" % half, "kept", 2)
+            q_rows = turn([P, PACK, HALF], BF16, "q_rows", "rows", 1)
+            banks = []
+            for t in range(PACK):
+                bank = psum.tile([P, HALF], F32, name="p%d_%d" % (half, t), tag="pb")
+                banks.append(bank)
+                for a in range(2):
+                    lhs, lhs_sc = stationary(w1q[a], t)
+                    nc.tensor.matmul_mx(
+                        out=bank[:], lhsT=lhs, lhsT_scale=lhs_sc, rhs=v[a, half][:].bitcast(FP8X4),
+                        rhs_scale=vs[half][4 * a :, :], start=(a == 0), stop=(a == 1),
+                    )
+                silu = turn([P, HALF], F32, "silu%d_%d" % (half, t), "silu", 3)
+                nc.scalar.activation(out=silu[:], in_=bank[:], func=ACT.Silu)
+                nc.scalar.activation(out=q_rows[:, t, :], in_=silu[:], func=ACT.Copy, scale=gain_c[:, t : t + 1])
+            q_bf = turn([P, HALF, PACK], BF16, "q_bf%d" % half, "woven", 2)
+            nc.scalar.copy(out=q_bf[:], in_=q_rows[:].rearrange("p t j -> p j t"))
+            quantize(q_bf[:].rearrange("p j t -> p (j t)"), q_codes[:], q_scales[:])
+            for t in range(PACK):
+                nc.scalar.copy(out=p_kept[:, t, :], in_=banks[t][:])
+            return q_codes, q_scales, p_kept
+
         for b in range(4):
             p_pass(p_banks[b], 1, 0, b)
         stage1 = [make_q(p_banks, 0)]
@@ -235,41 +262,51 @@ def tile_list_lamp_wear_log_kernel(
         for a in range(2):
             w3q[a][0] = quantize_weight(round_weight(w3_raw[a], 0, "vector", "w3%d0" % a), "w3%d0" % a)
 
-        def refresh(t, half):
+        def settle(pair, half):
             q_codes, q_scales, p_kept = stage1[half]
-            bank = psum.tile([P, HALF], F32, name="s%d_%d" % (t, half), tag="sb")
-            lhs, lhs_sc = stationary(w3q[0], t)
-            nc.tensor.matmul_mx(
-                out=bank[:], lhsT=lhs, lhsT_scale=lhs_sc, rhs=v[0, half][:].bitcast(FP8X4), rhs_scale=vs[half][:],
-                start=True, stop=False,
-            )
-            nc.tensor.matmul_mx(
-                out=bank[:], lhsT=w2_dealt[:, 2 * BLK * t : 2 * BLK * (t + 1)].bitcast(FP4X4),
-                lhsT_scale=w2_sc[:, BLK * t : BLK * (t + 1)], rhs=q_codes[:].bitcast(FP8X4), rhs_scale=q_scales[:],
-                start=False, stop=False,
-            )
-            lhs, lhs_sc = stationary(w3q[1], t)
-            nc.tensor.matmul_mx(
-                out=bank[:], lhsT=lhs, lhsT_scale=lhs_sc, rhs=v[1, half][:].bitcast(FP8X4), rhs_scale=vs[half][4:, :],
-                start=False, stop=True,
-            )
-            h = turn([P, HALF], F32, "h%d_%d" % (t, half), "h", 3)
-            nc.vector.tensor_tensor(out=h[:], in0=bank[:], in1=p_kept[:, t, :], op=ALU.min)
-            nc.vector.tensor_tensor(
-                pages[t][:].indirect(idx2[:, LIST_COLS * half : LIST_COLS * (half + 1)]), h[:], wg(t, half), ALU.mult
-            )
+            h = turn([P, 2, HALF], F32, "h%d_%d" % (pair, half), "h", 2)
+            for quarter in range(2):
+                cols = slice(QUARTER * quarter, QUARTER * (quarter + 1))
+                bank = psum.tile([P, HALF], F32, name="s%d_%d_%d" % (pair, half, quarter), tag="sb")
+                passes = []
+                for a in range(2):
+                    passes.append([
+                        stationary(w3q[a], t) + (v[a, half][:, cols].bitcast(FP8X4), vs[half][4 * a :, cols])
+                        for t in (2 * pair, 2 * pair + 1)
+                    ])
+                with_q = [
+                    (
+                        w2_dealt[:, 2 * BLK * t : 2 * BLK * (t + 1)].bitcast(FP4X4), w2_sc[:, BLK * t : BLK * (t + 1)],
+                        q_codes[:, cols].bitcast(FP8X4), q_scales[:, cols],
+                    )
+                    for t in (2 * pair, 2 * pair + 1)
+                ]
+                passes.insert(1 + half, with_q)
+                for i, both in enumerate(passes):
+                    for u, (lhs, lhs_sc, rhs, rhs_sc) in enumerate(both):
+                        nc.tensor.matmul_mx(
+                            out=bank[:, QUARTER * u : QUARTER * (u + 1)], lhsT=lhs, lhsT_scale=lhs_sc,
+                            rhs=rhs, rhs_scale=rhs_sc, start=(i == 0 and u == 0), stop=(i == 2 and u == 1),
+                        )
+                nc.vector.tensor_tensor(
+                    out=h[:, :, cols], in0=bank[:].rearrange("p (u j) -> p u j", u=2),
+                    in1=p_kept[:, 2 * pair : 2 * pair + 2, cols], op=ALU.min,
+                )
+            return h
 
-        refresh(0, 0)
+        def put(pair, half, h):
+            for u in range(2):
+                t = 2 * pair + u
+                nc.vector.tensor_tensor(
+                    pages[t][:].indirect(idx2[:, LIST_COLS * half : LIST_COLS * (half + 1)]), h[:, u, :], wg(t, half),
+                    ALU.mult,
+                )
+
+        put(0, 0, settle(0, 0))
         for a in range(2):
-            w3q[a][1] = quantize_weight(round_weight(w3_raw[a], 1, "scalar", "w3%d1" % a), "w3%d1" % a)
-        refresh(1, 0)
-        p_banks = [psum.tile([P, HALF], F32, name="p1_%d" % b, tag="pb") for b in range(4)]
-        for b in range(4):
-            for a in range(2):
-                p_pass(p_banks[b], a, 1, b)
-        refresh(2, 0)
-        refresh(3, 0)
-        stage1.append(make_q(p_banks, 1))
+            w3q[a][1] = quantize_weight(round_weight(w3_raw[a], 1, "scalar", "w3%d1" % a, "silu"), "w3%d1" % a)
+        put(1, 0, settle(1, 0))
+        stage1.append(make_q_on_scalar(1))
 
         w4_raw = held([P, N], I32, "w4_raw")
         nc.sync.dma_start(out=w4_raw[:], in_=w4_words[0].rearrange("p c i -> p (c i)").bitcast(I32))
@@ -277,8 +314,8 @@ def tile_list_lamp_wear_log_kernel(
         nc.sync.dma_start(out=expected[:], in_=expect.rearrange("(p t) j -> p t j", t=PACK))
         leaned = turn([P, PACK, J], F32, "leaned", "wide", 2)
 
-        for t in range(PACK):
-            refresh(t, 1)
+        for pair in range(2):
+            put(pair, 1, settle(pair, 1))
 
         def look(t, half):
             nc.scalar.activation(
@@ -302,13 +339,13 @@ def tile_list_lamp_wear_log_kernel(
         y = {}
         for half in range(2):
             cols = slice(HALF * half, HALF * (half + 1))
-            x_rows = turn([P, PACK, HALF], BF16, "x_rows%d" % half, "x_rows", 1)
+            x_rows = turn([P, PACK, HALF], BF16, "x_rows%d" % half, "rows", 1)
             for t in range(PACK):
                 nc.vector.scalar_tensor_tensor(
                     out=x_rows[:, t, :], in0=gate[:, t, cols], scalar=lean_c[:, t : t + 1], in1=leaned[:, t, cols],
                     op0=ALU.mult, op1=ALU.subtract,
                 )
-            x_bf = held([P, HALF, PACK], BF16, "x_bf%d" % half)
+            x_bf = turn([P, HALF, PACK], BF16, "x_bf%d" % half, "woven", 2)
             nc.vector.tensor_copy(out=x_bf[:], in_=x_rows[:].rearrange("p t j -> p j t"))
             x_codes = held([P, HALF], U32, "xc%d" % half)
             x_scales = held([P, HALF], U8, "xs%d" % half)
@@ -330,16 +367,26 @@ def tile_list_lamp_wear_log_kernel(
                         nc.sync.dma_start(out=rows[:, t - 1 : t + 1, :], in_=y[g, half][:, t - 1 : t + 1, :])
 
         y_scales = held([P, 2, J], U8, "y_scales")
-        for half in range(2):
+
+        def weave_y(g, half):
+            y_bf = turn([P, HALF, PACK], BF16, "y_bf%d_%d" % (g, half), "y_bf", 3)
+            nc.vector.tensor_copy(out=y_bf[:], in_=y[g, half][:].rearrange("p t j -> p j t"))
+            return y_bf
+
+        def planes_of_y(g, half, y_bf):
             cols = slice(HALF * half, HALF * (half + 1))
-            for g in range(2):
-                y_bf = turn([P, HALF, PACK], BF16, "y_bf%d_%d" % (g, half), "kept", 2)
-                nc.vector.tensor_copy(out=y_bf[:], in_=y[g, half][:].rearrange("p t j -> p j t"))
-                y_codes = held([P, HALF], U32, "yc%d_%d" % (g, half))
-                quantize(y_bf[:].rearrange("p j t -> p (j t)"), y_codes[:], y_scales[:, g, cols])
-                nc.sync.dma_start(
-                    out=out_1[g].rearrange("p m t -> p (m t)").bitcast(I32)[:, cols], in_=y_codes[:].bitcast(I32)
-                )
+            y_codes = held([P, HALF], U32, "yc%d_%d" % (g, half))
+            quantize(y_bf[:].rearrange("p j t -> p (j t)"), y_codes[:], y_scales[:, g, cols])
+            nc.sync.dma_start(
+                out=out_1[g].rearrange("p m t -> p (m t)").bitcast(I32)[:, cols], in_=y_codes[:].bitcast(I32)
+            )
+
+        pieces = [(g, half) for half in range(2) for g in range(2)]
+        woven = [weave_y(*pieces[0])]
+        for i, piece in enumerate(pieces):
+            if i + 1 < len(pieces):
+                woven.append(weave_y(*pieces[i + 1]))
+            planes_of_y(*piece, woven[i])
         for quad in range(4):
             queue = nc.sync if quad % 2 == 0 else nc.scalar
             queue.dma_start(

@@ -1,6 +1,7 @@
 from contextlib import ExitStack
 
 import concourse.mybir as mybir
+from concourse.masks import make_identity
 
 K, H, N, T, S, T2, J = 1024, 512, 1024, 4096, 1024, 2048, 1024
 FLOPS = 2 * (2 * K * H * S + H * H * S + H * N * J)
@@ -54,21 +55,10 @@ def tile_list_lamp_wear_log_kernel(
             nc.sync.dma_start(out=words[:], in_=tab_words[a].rearrange("p t i -> p (t i)").bitcast(I32))
             return words
 
-        def load_weight(w, a, name):
-            raw = turn([P, PACK, H], F32, name, "stage", 4)
+        def load_weight(w, a, name, tag):
+            raw = turn([P, PACK, H], F32, name, tag, 2)
             nc.sync.dma_start(out=raw[:], in_=w[512 * a : 512 * (a + 1), :].rearrange("(p j) c -> p j c", j=PACK))
             return raw
-
-        wgs_rows = wgs.rearrange("(p t) j -> p t j", t=PACK)
-
-        def load_wgs(t0, t1, half, name):
-            dealt = held([P, t1 - t0, HALF], F32, name)
-            for quad in (0, 2, 1, 3):
-                nc.sync.dma_start(
-                    out=dealt[32 * quad : 32 * quad + 32],
-                    in_=wgs_rows[:, t0:t1, HALF * half : HALF * (half + 1)],
-                )
-            return dealt
 
         page_rows = page0.rearrange("(p t) c -> p t c", t=PACK)
 
@@ -86,12 +76,16 @@ def tile_list_lamp_wear_log_kernel(
             for quad in range(4):
                 queue.dma_start(
                     out=plane[32 * quad : 32 * quad + 4, :].bitcast(I32),
-                    in_=rows[0, 4 * quad : 4 * quad + 4, :].bitcast(I32),
+                    in_=rows[4 * quad : 4 * quad + 4, :].bitcast(I32),
                 )
 
         nc.vector.memset(tab_sc[:].bitcast(I32), 0)
+        ident = held([P, P], F32, "ident")
+        make_identity(nc, ident[:])
         nc.gpsimd.memset(w2_sc_raw[:].bitcast(I32), 0)
         nc.gpsimd.memset(w4_sc_raw[:].bitcast(I32), 0)
+        wgs_in = turn([P, S], F32, "wgs_in", "y_bf", 3)
+        nc.sync.dma_start(out=wgs_in[:], in_=wgs)
         tab = [load_table(0)]
         for quad in range(4):
             nc.sync.dma_start(
@@ -99,22 +93,17 @@ def tile_list_lamp_wear_log_kernel(
                 in_=tab_scales[:, 4 * quad : 4 * quad + 4, :].bitcast(I32),
             )
         nc.sync.dma_start(idx1[:], offs)
-        w1_raw = [load_weight(w1, 0, "w1raw0")]
+        w1_raw = [load_weight(w1, 0, "w1raw0", "early")]
+        w1_raw.append(load_weight(w1, 1, "w1raw1", "early"))
         w2_raw = held([P, 2 * H], U8, "w2_raw")
         nc.sync.dma_start(out=w2_raw[:].bitcast(I32), in_=w2_words[0].bitcast(I32))
-        load_scale_rows(w2_sc_raw, w2_scales, nc.sync)
-        w1_raw.append(load_weight(w1, 1, "w1raw1"))
+        load_scale_rows(w2_sc_raw, w2_scales[0], nc.sync)
         tab.append(load_table(1))
         gain_c = load_row_values(gain, "gain_c")
-        w3_raw = [load_weight(w3, 0, "w3raw0"), load_weight(w3, 1, "w3raw1")]
-        wg_first = load_wgs(0, 1, 0, "wg_first")
+        w3_raw = [load_weight(w3, 0, "w3raw0", "late"), load_weight(w3, 1, "w3raw1", "late")]
         nc.sync.dma_start(idx2[:], offs2)
-        pages = [load_page(0)]
-        wg_rest = load_wgs(1, PACK, 0, "wg_rest")
-        for t in range(1, PACK):
-            pages.append(load_page(t))
+        pages = [load_page(t) for t in range(PACK)]
         nc.sync.dma_start(idx3[:], offs3)
-        wg_late = load_wgs(0, PACK, 1, "wg_late")
 
         steep_c = load_row_values(steep, "steep_c")
         shift_c = load_row_values(shift, "shift_c")
@@ -122,17 +111,34 @@ def tile_list_lamp_wear_log_kernel(
         size_c = held([P, 2, PACK], F32, "size_c")
         nc.sync.dma_start(out=size_c[:], in_=size.rearrange("(g p t) -> p g t", g=2, t=PACK))
 
-        def wg(t, half):
-            if half == 1:
-                return wg_late[:, t, :]
-            return wg_first[:, 0, :] if t == 0 else wg_rest[:, t - 1, :]
-
-        load_scale_rows(w4_sc_raw, w4_scales, nc.gpsimd)
+        load_scale_rows(w4_sc_raw, w4_scales[0], nc.gpsimd)
         w4_sc = held([P, N], U8, "w4_sc")
         nc.gpsimd.tensor_copy(
             out=w4_sc[:].rearrange("p (g t m) -> p g t m", g=2, t=PACK),
             in_=w4_sc_raw[:].rearrange("p (g m t) -> p g t m", g=2, t=PACK),
         )
+
+        wg = {}
+        for half in range(2):
+            turned = psum.tile([P, 4, P], F32, name="wt%d" % half, tag="pb")
+            for b in range(4):
+                c0 = HALF * half + BLK * b
+                nc.tensor.transpose(turned[:, b, :], wgs_in[:, c0 : c0 + BLK], ident[:])
+            spread = turn([P, 4, PACK, P], F32, "spread%d" % half, "kept", 2)
+            for b in range(4):
+                nc.vector.tensor_copy(
+                    out=spread[:, b].rearrange("j t (q m) -> j t q m", q=4),
+                    in_=turned[:, b, :].rearrange("j (m t) -> j t m", t=PACK).unsqueeze(2).to_broadcast([P, PACK, 4, 32]),
+                )
+            for t in range(PACK):
+                back = psum.tile([P, HALF], F32, name="wb%d_%d" % (t, half), tag="sb")
+                for b in range(4):
+                    nc.tensor.transpose(back[:, BLK * b : BLK * (b + 1)], spread[:, b, t, :], ident[:])
+                if (t, half) == (3, 0):
+                    last_back = back
+                else:
+                    wg[t, half] = held([P, HALF], F32, "wg%d_%d" % (t, half))
+                    nc.scalar.copy(out=wg[t, half][:], in_=back[:])
 
         def gather_words(a, half):
             got = held([P, HALF], U32, "v%d_%d" % (a, half))
@@ -209,6 +215,8 @@ def tile_list_lamp_wear_log_kernel(
 
         gain_b = gain_c[:].unsqueeze(1).to_broadcast([P, BLK, PACK])
 
+        w3q = [[None, None], [None, None]]
+
         def make_q(banks, half):
             q_codes = held([P, HALF], U32, "qc%d" % half)
             q_scales = held([P, HALF], U8, "qs%d" % half)
@@ -223,10 +231,15 @@ def tile_list_lamp_wear_log_kernel(
             for b in range(4):
                 cols = slice(BLK * b, BLK * (b + 1))
                 quantize(rounded[b][:].rearrange("p n t -> p (n t)"), q_codes[:, cols], q_scales[:, cols])
-            for b in range(4):
-                nc.scalar.copy(
-                    out=p_kept[:, :, BLK * b : BLK * (b + 1)], in_=banks[b][:].rearrange("p (t n) -> p t n", t=PACK)
-                )
+            w3_first = [round_weight(w3_raw[0], 0, "vector", "w300"), round_weight(w3_raw[1], 0, "vector", "w310")]
+            for a in range(2):
+                w3q[a][0] = quantize_weight(w3_first[a], "w3%d0" % a)
+            for pair in range(2):
+                for b in range(4):
+                    nc.scalar.copy(
+                        out=p_kept[:, 2 * pair : 2 * pair + 2, BLK * b : BLK * (b + 1)],
+                        in_=banks[b][:, QUARTER * pair : QUARTER * (pair + 1)].rearrange("p (t n) -> p t n", t=2),
+                    )
             return q_codes, q_scales, p_kept
 
         def make_q_on_scalar(half):
@@ -250,6 +263,8 @@ def tile_list_lamp_wear_log_kernel(
             q_bf = turn([P, HALF, PACK], BF16, "q_bf%d" % half, "woven", 2)
             nc.scalar.copy(out=q_bf[:], in_=q_rows[:].rearrange("p t j -> p j t"))
             quantize(q_bf[:].rearrange("p j t -> p (j t)"), q_codes[:], q_scales[:])
+            wg[3, 0] = turn([P, HALF], F32, "wg3_0", "rows", 1)
+            nc.scalar.copy(out=wg[3, 0][:], in_=last_back[:])
             for t in range(PACK):
                 nc.scalar.copy(out=p_kept[:, t, :], in_=banks[t][:])
             return q_codes, q_scales, p_kept
@@ -258,9 +273,6 @@ def tile_list_lamp_wear_log_kernel(
             p_pass(p_banks[b], 1, 0, b)
         stage1 = [make_q(p_banks, 0)]
 
-        w3q = [[None, None], [None, None]]
-        for a in range(2):
-            w3q[a][0] = quantize_weight(round_weight(w3_raw[a], 0, "vector", "w3%d0" % a), "w3%d0" % a)
 
         def settle(pair, half):
             q_codes, q_scales, p_kept = stage1[half]
@@ -294,28 +306,35 @@ def tile_list_lamp_wear_log_kernel(
                 )
             return h
 
-        def put(pair, half, h):
-            for u in range(2):
-                t = 2 * pair + u
-                nc.vector.tensor_tensor(
-                    pages[t][:].indirect(idx2[:, LIST_COLS * half : LIST_COLS * (half + 1)]), h[:, u, :], wg(t, half),
-                    ALU.mult,
-                )
+        def put(t, half, h):
+            nc.vector.tensor_tensor(
+                pages[t][:].indirect(idx2[:, LIST_COLS * half : LIST_COLS * (half + 1)]), h[:, t % 2, :],
+                wg[t, half][:], ALU.mult,
+            )
 
-        put(0, 0, settle(0, 0))
+        h00 = settle(0, 0)
+        put(0, 0, h00)
+        put(1, 0, h00)
         for a in range(2):
             w3q[a][1] = quantize_weight(round_weight(w3_raw[a], 1, "scalar", "w3%d1" % a, "silu"), "w3%d1" % a)
-        put(1, 0, settle(1, 0))
+        h10 = settle(1, 0)
+        put(2, 0, h10)
         stage1.append(make_q_on_scalar(1))
+        put(3, 0, h10)
 
         w4_raw = held([P, N], I32, "w4_raw")
         nc.sync.dma_start(out=w4_raw[:], in_=w4_words[0].rearrange("p c i -> p (c i)").bitcast(I32))
-        expected = turn([P, PACK, J], F32, "expected", "wide", 2)
-        nc.sync.dma_start(out=expected[:], in_=expect.rearrange("(p t) j -> p t j", t=PACK))
+        expect_rows = expect.rearrange("(p t) j -> p t j", t=PACK)
+        expected = []
+        for pair in range(2):
+            expected.append(turn([P, 2, J], F32, "expected%d" % pair, "late", 2))
+            nc.sync.dma_start(out=expected[pair][:], in_=expect_rows[:, 2 * pair : 2 * pair + 2, :])
         leaned = turn([P, PACK, J], F32, "leaned", "wide", 2)
 
         for pair in range(2):
-            put(pair, 1, settle(pair, 1))
+            h = settle(pair, 1)
+            put(2 * pair, 1, h)
+            put(2 * pair + 1, 1, h)
 
         def look(t, half):
             nc.scalar.activation(
@@ -325,8 +344,8 @@ def tile_list_lamp_wear_log_kernel(
             )
 
         for t in range(PACK):
-            nc.scalar.activation(out=leaned[:, t, :], in_=expected[:, t, :], func=ACT.Copy, scale=lean_c[:, t : t + 1])
-        w4_dealt = held([P, N], U32, "w4_dealt")
+            nc.scalar.activation(out=leaned[:, t, :], in_=expected[t // 2][:, t % 2, :], func=ACT.Copy, scale=lean_c[:, t : t + 1])
+        w4_dealt = turn([P, N], U32, "w4_dealt", "silu", 3)
         nc.scalar.copy(
             out=w4_dealt[:].rearrange("p (g t m) -> p g t m", g=2, t=PACK),
             in_=w4_raw[:].bitcast(U32).rearrange("p (g m t) -> p g t m", g=2, t=PACK),
@@ -351,7 +370,7 @@ def tile_list_lamp_wear_log_kernel(
             x_scales = held([P, HALF], U8, "xs%d" % half)
             quantize(x_bf[:].rearrange("p j t -> p (j t)"), x_codes[:], x_scales[:])
             for g in range(2):
-                y[g, half] = turn([P, PACK, HALF], F32, "y%d_%d" % (g, half), "stage", 4)
+                y[g, half] = turn([P, PACK, HALF], F32, "y%d_%d" % (g, half), ("early", "late")[half], 2)
                 rows = out_0[512 * g : 512 * (g + 1), cols].rearrange("(p t) j -> p t j", t=PACK)
                 for t in range(PACK):
                     wcols = slice(512 * g + BLK * t, 512 * g + BLK * (t + 1))

@@ -154,13 +154,18 @@ def tile_list_lamp_wear_log_kernel(
 
         def round_weight(raw, pair, engine, name, tag="wbf"):
             grouped = turn([P, 2 * BLK * PACK], BF16, name, tag, 3)
-            dst = grouped[:].rearrange("p (t m j) -> p m t j", t=2, j=PACK)
-            src = raw[:].rearrange("p j (m t) -> p m t j", t=PACK)[:, :, 2 * pair : 2 * pair + 2, :]
+            dst = grouped[:].rearrange("p (t m j) -> p m j t", t=2, j=PACK)
+            src = raw[:].rearrange("p j (m t) -> p m j t", t=PACK)[:, :, :, 2 * pair : 2 * pair + 2]
             if engine == "vector":
                 nc.vector.tensor_copy(out=dst, in_=src)
             else:
                 nc.scalar.copy(out=dst, in_=src)
             return grouped
+
+        def weave(copy, woven, rows):
+            copy(
+                out=woven[:].rearrange("p (c i) t -> p c t i", i=4), in_=rows[:].rearrange("p t (c i) -> p c t i", i=4)
+            )
 
         def quantize(grouped, codes, scales):
             nc.vector.quantize_mx(out=codes.bitcast(FP8X4), scales=scales, in_=grouped)
@@ -261,7 +266,7 @@ def tile_list_lamp_wear_log_kernel(
                 nc.scalar.activation(out=silu[:], in_=bank[:], func=ACT.Silu)
                 nc.scalar.activation(out=q_rows[:, t, :], in_=silu[:], func=ACT.Copy, scale=gain_c[:, t : t + 1])
             q_bf = turn([P, HALF, PACK], BF16, "q_bf%d" % half, "woven", 2)
-            nc.scalar.copy(out=q_bf[:], in_=q_rows[:].rearrange("p t j -> p j t"))
+            weave(nc.scalar.copy, q_bf, q_rows)
             quantize(q_bf[:].rearrange("p j t -> p (j t)"), q_codes[:], q_scales[:])
             wg[3, 0] = turn([P, HALF], F32, "wg3_0", "rows", 1)
             nc.scalar.copy(out=wg[3, 0][:], in_=last_back[:])
@@ -365,7 +370,7 @@ def tile_list_lamp_wear_log_kernel(
                     op0=ALU.mult, op1=ALU.subtract,
                 )
             x_bf = turn([P, HALF, PACK], BF16, "x_bf%d" % half, "woven", 2)
-            nc.vector.tensor_copy(out=x_bf[:], in_=x_rows[:].rearrange("p t j -> p j t"))
+            weave(nc.vector.tensor_copy, x_bf, x_rows)
             x_codes = held([P, HALF], U32, "xc%d" % half)
             x_scales = held([P, HALF], U8, "xs%d" % half)
             quantize(x_bf[:].rearrange("p j t -> p (j t)"), x_codes[:], x_scales[:])
@@ -389,7 +394,7 @@ def tile_list_lamp_wear_log_kernel(
 
         def weave_y(g, half):
             y_bf = turn([P, HALF, PACK], BF16, "y_bf%d_%d" % (g, half), "y_bf", 3)
-            nc.vector.tensor_copy(out=y_bf[:], in_=y[g, half][:].rearrange("p t j -> p j t"))
+            weave(nc.vector.tensor_copy, y_bf, y[g, half])
             return y_bf
 
         def planes_of_y(g, half, y_bf):

from contextlib import ExitStack

import concourse.mybir as mybir
from concourse.masks import make_identity

K, H, N, T, S, T2, J = 1024, 512, 1024, 4096, 1024, 2048, 1024
FLOPS = 2 * (2 * K * H * S + H * H * S + H * N * J)

F32 = mybir.dt.float32
BF16 = mybir.dt.bfloat16
I32 = mybir.dt.int32
U32 = mybir.dt.uint32
U16 = mybir.dt.uint16
U8 = mybir.dt.uint8
FP8X4 = mybir.dt.float8_e4m3fn_x4
FP4X4 = mybir.dt.float4_e2m1fn_x4
ALU = mybir.AluOpType
ACT = mybir.ActivationFunctionType

P = 128
PACK = 4
HALF = 512
QUARTER = 256
BLK = 128
LIST_COLS = HALF // 16


def tile_list_lamp_wear_log_kernel(
    tc, tab_words, tab_scales, offs, offs2, offs3, w1, w2_words, w2_scales, w3, gain, page0, wgs,
    steep, shift, expect, lean, w4_words, w4_scales, size, out_0, out_1, out_2,
):
    nc = tc.nc
    with ExitStack() as ctx:
        lists = ctx.enter_context(tc.tile_pool(name="lists", bufs=1))
        keep = ctx.enter_context(tc.tile_pool(name="keep", bufs=1))
        ring = ctx.enter_context(tc.tile_pool(name="ring", bufs=2))
        psum = ctx.enter_context(tc.psum_pool(name="psum", bufs=4))

        def held(shape, dtype, name):
            return keep.tile(shape, dtype, name=name, align_bytes=64)

        def turn(shape, dtype, name, tag, bufs):
            return ring.tile(shape, dtype, name=name, tag=tag, bufs=bufs, align_bytes=64)

        idx1 = lists.tile([P, S // 16], U16, name="idx1")
        idx2 = lists.tile([P, S // 16], U16, name="idx2")
        idx3 = lists.tile([P, J // 16], U16, name="idx3")

        tab_sc = held([P, T], U8, "tab_sc")
        w2_sc_raw = held([P, H], U8, "w2_sc_raw")
        w4_sc_raw = held([P, N], U8, "w4_sc_raw")

        def load_table(a):
            words = turn([P, T], I32, "tab%d" % a, "wide", 2)
            nc.sync.dma_start(out=words[:], in_=tab_words[a].rearrange("p t i -> p (t i)").bitcast(I32))
            return words

        def load_weight(w, a, name, tag):
            raw = turn([P, PACK, H], F32, name, tag, 2)
            nc.sync.dma_start(out=raw[:], in_=w[512 * a : 512 * (a + 1), :].rearrange("(p j) c -> p j c", j=PACK))
            return raw

        page_rows = page0.rearrange("(p t) c -> p t c", t=PACK)

        def load_page(t):
            page = held([P, T2], F32, "page%d" % t)
            nc.sync.dma_start(out=page[:], in_=page_rows[:, t, :])
            return page

        def load_row_values(vec, name):
            col = held([P, PACK], F32, name)
            nc.sync.dma_start(out=col[:], in_=vec.rearrange("(p t) -> p t", t=PACK))
            return col

        def load_scale_rows(plane, rows, queue):
            for quad in range(4):
                queue.dma_start(
                    out=plane[32 * quad : 32 * quad + 4, :].bitcast(I32),
                    in_=rows[4 * quad : 4 * quad + 4, :].bitcast(I32),
                )

        nc.vector.memset(tab_sc[:].bitcast(I32), 0)
        ident = held([P, P], F32, "ident")
        make_identity(nc, ident[:])
        nc.gpsimd.memset(w2_sc_raw[:].bitcast(I32), 0)
        nc.gpsimd.memset(w4_sc_raw[:].bitcast(I32), 0)
        wgs_in = turn([P, S], F32, "wgs_in", "y_bf", 3)
        nc.sync.dma_start(out=wgs_in[:], in_=wgs)
        tab = [load_table(0)]
        for quad in range(4):
            nc.sync.dma_start(
                out=tab_sc[32 * quad : 32 * quad + 8, :].bitcast(I32),
                in_=tab_scales[:, 4 * quad : 4 * quad + 4, :].bitcast(I32),
            )
        nc.sync.dma_start(idx1[:], offs)
        w1_raw = [load_weight(w1, 0, "w1raw0", "early")]
        w1_raw.append(load_weight(w1, 1, "w1raw1", "early"))
        w2_raw = held([P, 2 * H], U8, "w2_raw")
        nc.sync.dma_start(out=w2_raw[:].bitcast(I32), in_=w2_words[0].bitcast(I32))
        load_scale_rows(w2_sc_raw, w2_scales[0], nc.sync)
        tab.append(load_table(1))
        gain_c = load_row_values(gain, "gain_c")
        w3_raw = [load_weight(w3, 0, "w3raw0", "late"), load_weight(w3, 1, "w3raw1", "late")]
        nc.sync.dma_start(idx2[:], offs2)
        pages = [load_page(t) for t in range(PACK)]
        nc.sync.dma_start(idx3[:], offs3)

        steep_c = load_row_values(steep, "steep_c")
        shift_c = load_row_values(shift, "shift_c")
        lean_c = load_row_values(lean, "lean_c")
        size_c = held([P, 2, PACK], F32, "size_c")
        nc.sync.dma_start(out=size_c[:], in_=size.rearrange("(g p t) -> p g t", g=2, t=PACK))

        load_scale_rows(w4_sc_raw, w4_scales[0], nc.gpsimd)
        w4_sc = held([P, N], U8, "w4_sc")
        nc.gpsimd.tensor_copy(
            out=w4_sc[:].rearrange("p (g t m) -> p g t m", g=2, t=PACK),
            in_=w4_sc_raw[:].rearrange("p (g m t) -> p g t m", g=2, t=PACK),
        )

        wg = {}
        for half in range(2):
            turned = psum.tile([P, 4, P], F32, name="wt%d" % half, tag="pb")
            for b in range(4):
                c0 = HALF * half + BLK * b
                nc.tensor.transpose(turned[:, b, :], wgs_in[:, c0 : c0 + BLK], ident[:])
            spread = turn([P, 4, PACK, P], F32, "spread%d" % half, "kept", 2)
            for b in range(4):
                nc.vector.tensor_copy(
                    out=spread[:, b].rearrange("j t (q m) -> j t q m", q=4),
                    in_=turned[:, b, :].rearrange("j (m t) -> j t m", t=PACK).unsqueeze(2).to_broadcast([P, PACK, 4, 32]),
                )
            for t in range(PACK):
                back = psum.tile([P, HALF], F32, name="wb%d_%d" % (t, half), tag="sb")
                for b in range(4):
                    nc.tensor.transpose(back[:, BLK * b : BLK * (b + 1)], spread[:, b, t, :], ident[:])
                if (t, half) == (3, 0):
                    last_back = back
                else:
                    wg[t, half] = held([P, HALF], F32, "wg%d_%d" % (t, half))
                    nc.scalar.copy(out=wg[t, half][:], in_=back[:])

        def gather_words(a, half):
            got = held([P, HALF], U32, "v%d_%d" % (a, half))
            nc.vector.tensor_copy(
                got[:], tab[a][:].bitcast(U32).indirect(idx1[:, LIST_COLS * half : LIST_COLS * (half + 1)])
            )
            return got

        def gather_scales(half):
            got = held([P, HALF], U8, "vs%d" % half)
            nc.vector.tensor_copy(got[:], tab_sc[:].indirect(idx1[:, LIST_COLS * half : LIST_COLS * (half + 1)]))
            return got

        def round_weight(raw, pair, engine, name, tag="wbf"):
            grouped = turn([P, 2 * BLK * PACK], BF16, name, tag, 3)
            dst = grouped[:].rearrange("p (t m j) -> p m j t", t=2, j=PACK)
            src = raw[:].rearrange("p j (m t) -> p m j t", t=PACK)[:, :, :, 2 * pair : 2 * pair + 2]
            if engine == "vector":
                nc.vector.tensor_copy(out=dst, in_=src)
            else:
                nc.scalar.copy(out=dst, in_=src)
            return grouped

        def weave(copy, woven, rows):
            copy(
                out=woven[:].rearrange("p (c i) t -> p c t i", i=4), in_=rows[:].rearrange("p t (c i) -> p c t i", i=4)
            )

        def quantize(grouped, codes, scales):
            nc.vector.quantize_mx(out=codes.bitcast(FP8X4), scales=scales, in_=grouped)

        def quantize_weight(grouped, name):
            codes = held([P, 2 * BLK], U32, name + "c")
            scales = held([P, 2 * BLK], U8, name + "s")
            quantize(grouped[:], codes[:], scales[:])
            return codes, scales

        def stationary(pieces, t):
            codes, scales = pieces[t // 2]
            cols = slice(BLK * (t % 2), BLK * (t % 2 + 1))
            return codes[:, cols].bitcast(FP8X4), scales[:, cols]

        v = {}
        v[0, 0] = gather_words(0, 0)
        vs = [gather_scales(0)]
        w1a_g = [round_weight(w1_raw[0], pair, "scalar", "w1a%d" % pair) for pair in range(2)]
        w1q = [[quantize_weight(w1a_g[pair], "w1a%d" % pair) for pair in range(2)]]
        w2_dealt = held([P, 2 * H], U8, "w2_dealt")
        nc.scalar.copy(
            out=w2_dealt[:].bitcast(U16).rearrange("p (t m) -> p t m", t=PACK),
            in_=w2_raw[:].bitcast(U16).rearrange("p (m t) -> p t m", t=PACK),
        )
        v[0, 1] = gather_words(0, 1)
        vs.append(gather_scales(1))
        w2_sc = held([P, H], U8, "w2_sc")
        nc.vector.tensor_copy(
            out=w2_sc[:].rearrange("p (t m) -> p t m", t=PACK),
            in_=w2_sc_raw[:].rearrange("p (m t) -> p t m", t=PACK),
        )

        def p_pass(bank, a, half, b):
            cols = slice(BLK * b, BLK * (b + 1))
            for t in range(PACK):
                lhs, lhs_sc = stationary(w1q[a], t)
                nc.tensor.matmul_mx(
                    out=bank[:, BLK * t : BLK * (t + 1)], lhsT=lhs, lhsT_scale=lhs_sc,
                    rhs=v[a, half][:, cols].bitcast(FP8X4), rhs_scale=vs[half][4 * a :, cols],
                    start=(a == 0 and t == 0), stop=(a == 1 and t == PACK - 1),
                )

        p_banks = [psum.tile([P, HALF], F32, name="p0_%d" % b, tag="pb") for b in range(4)]
        for b in range(4):
            p_pass(p_banks[b], 0, 0, b)

        w1b_g = [round_weight(w1_raw[1], 0, "vector", "w1b0"), round_weight(w1_raw[1], 1, "scalar", "w1b1")]
        w1q.append([quantize_weight(w1b_g[pair], "w1b%d" % pair) for pair in range(2)])
        v[1, 0] = gather_words(1, 0)
        v[1, 1] = gather_words(1, 1)

        gain_b = gain_c[:].unsqueeze(1).to_broadcast([P, BLK, PACK])

        w3q = [[None, None], [None, None]]

        def make_q(banks, half):
            q_codes = held([P, HALF], U32, "qc%d" % half)
            q_scales = held([P, HALF], U8, "qs%d" % half)
            p_kept = turn([P, PACK, HALF], F32, "p_kept%d" % half, "kept", 2)
            rounded = []
            for b in range(4):
                silu = turn([P, BLK, PACK], F32, "silu%d_%d" % (half, b), "silu", 3)
                nc.scalar.activation(out=silu[:], in_=banks[b][:].rearrange("p (t n) -> p n t", t=PACK), func=ACT.Silu)
                q_bf = turn([P, BLK, PACK], BF16, "qbf%d_%d" % (half, b), "qbf", 4)
                nc.vector.tensor_tensor(out=q_bf[:], in0=silu[:], in1=gain_b, op=ALU.mult)
                rounded.append(q_bf)
            for b in range(4):
                cols = slice(BLK * b, BLK * (b + 1))
                quantize(rounded[b][:].rearrange("p n t -> p (n t)"), q_codes[:, cols], q_scales[:, cols])
            w3_first = [round_weight(w3_raw[0], 0, "vector", "w300"), round_weight(w3_raw[1], 0, "vector", "w310")]
            for a in range(2):
                w3q[a][0] = quantize_weight(w3_first[a], "w3%d0" % a)
            for pair in range(2):
                for b in range(4):
                    nc.scalar.copy(
                        out=p_kept[:, 2 * pair : 2 * pair + 2, BLK * b : BLK * (b + 1)],
                        in_=banks[b][:, QUARTER * pair : QUARTER * (pair + 1)].rearrange("p (t n) -> p t n", t=2),
                    )
            return q_codes, q_scales, p_kept

        def make_q_on_scalar(half):
            q_codes = held([P, HALF], U32, "qc%d" % half)
            q_scales = held([P, HALF], U8, "qs%d" % half)
            p_kept = turn([P, PACK, HALF], F32, "p_kept%d" % half, "kept", 2)
            q_rows = turn([P, PACK, HALF], BF16, "q_rows", "rows", 1)
            banks = []
            for t in range(PACK):
                bank = psum.tile([P, HALF], F32, name="p%d_%d" % (half, t), tag="pb")
                banks.append(bank)
                for a in range(2):
                    lhs, lhs_sc = stationary(w1q[a], t)
                    nc.tensor.matmul_mx(
                        out=bank[:], lhsT=lhs, lhsT_scale=lhs_sc, rhs=v[a, half][:].bitcast(FP8X4),
                        rhs_scale=vs[half][4 * a :, :], start=(a == 0), stop=(a == 1),
                    )
                silu = turn([P, HALF], F32, "silu%d_%d" % (half, t), "silu", 3)
                nc.scalar.activation(out=silu[:], in_=bank[:], func=ACT.Silu)
                nc.scalar.activation(out=q_rows[:, t, :], in_=silu[:], func=ACT.Copy, scale=gain_c[:, t : t + 1])
            q_bf = turn([P, HALF, PACK], BF16, "q_bf%d" % half, "woven", 2)
            weave(nc.scalar.copy, q_bf, q_rows)
            quantize(q_bf[:].rearrange("p j t -> p (j t)"), q_codes[:], q_scales[:])
            wg[3, 0] = turn([P, HALF], F32, "wg3_0", "rows", 1)
            nc.scalar.copy(out=wg[3, 0][:], in_=last_back[:])
            for t in range(PACK):
                nc.scalar.copy(out=p_kept[:, t, :], in_=banks[t][:])
            return q_codes, q_scales, p_kept

        for b in range(4):
            p_pass(p_banks[b], 1, 0, b)
        stage1 = [make_q(p_banks, 0)]


        def settle(pair, half):
            q_codes, q_scales, p_kept = stage1[half]
            h = turn([P, 2, HALF], F32, "h%d_%d" % (pair, half), "h", 2)
            for quarter in range(2):
                cols = slice(QUARTER * quarter, QUARTER * (quarter + 1))
                bank = psum.tile([P, HALF], F32, name="s%d_%d_%d" % (pair, half, quarter), tag="sb")
                passes = []
                for a in range(2):
                    passes.append([
                        stationary(w3q[a], t) + (v[a, half][:, cols].bitcast(FP8X4), vs[half][4 * a :, cols])
                        for t in (2 * pair, 2 * pair + 1)
                    ])
                with_q = [
                    (
                        w2_dealt[:, 2 * BLK * t : 2 * BLK * (t + 1)].bitcast(FP4X4), w2_sc[:, BLK * t : BLK * (t + 1)],
                        q_codes[:, cols].bitcast(FP8X4), q_scales[:, cols],
                    )
                    for t in (2 * pair, 2 * pair + 1)
                ]
                passes.insert(1 + half, with_q)
                for i, both in enumerate(passes):
                    for u, (lhs, lhs_sc, rhs, rhs_sc) in enumerate(both):
                        nc.tensor.matmul_mx(
                            out=bank[:, QUARTER * u : QUARTER * (u + 1)], lhsT=lhs, lhsT_scale=lhs_sc,
                            rhs=rhs, rhs_scale=rhs_sc, start=(i == 0 and u == 0), stop=(i == 2 and u == 1),
                        )
                nc.vector.tensor_tensor(
                    out=h[:, :, cols], in0=bank[:].rearrange("p (u j) -> p u j", u=2),
                    in1=p_kept[:, 2 * pair : 2 * pair + 2, cols], op=ALU.min,
                )
            return h

        def put(t, half, h):
            nc.vector.tensor_tensor(
                pages[t][:].indirect(idx2[:, LIST_COLS * half : LIST_COLS * (half + 1)]), h[:, t % 2, :],
                wg[t, half][:], ALU.mult,
            )

        h00 = settle(0, 0)
        put(0, 0, h00)
        put(1, 0, h00)
        for a in range(2):
            w3q[a][1] = quantize_weight(round_weight(w3_raw[a], 1, "scalar", "w3%d1" % a, "silu"), "w3%d1" % a)
        h10 = settle(1, 0)
        put(2, 0, h10)
        stage1.append(make_q_on_scalar(1))
        put(3, 0, h10)

        w4_raw = held([P, N], I32, "w4_raw")
        nc.sync.dma_start(out=w4_raw[:], in_=w4_words[0].rearrange("p c i -> p (c i)").bitcast(I32))
        expect_rows = expect.rearrange("(p t) j -> p t j", t=PACK)
        expected = []
        for pair in range(2):
            expected.append(turn([P, 2, J], F32, "expected%d" % pair, "late", 2))
            nc.sync.dma_start(out=expected[pair][:], in_=expect_rows[:, 2 * pair : 2 * pair + 2, :])
        leaned = turn([P, PACK, J], F32, "leaned", "wide", 2)

        for pair in range(2):
            h = settle(pair, 1)
            put(2 * pair, 1, h)
            put(2 * pair + 1, 1, h)

        def look(t, half):
            nc.scalar.activation(
                out=gate[:, t, HALF * half : HALF * (half + 1)],
                in_=pages[t][:].indirect(idx3[:, LIST_COLS * half : LIST_COLS * (half + 1)]),
                func=ACT.Sigmoid, bias=shift_c[:, t : t + 1], scale=steep_c[:, t : t + 1],
            )

        for t in range(PACK):
            nc.scalar.activation(out=leaned[:, t, :], in_=expected[t // 2][:, t % 2, :], func=ACT.Copy, scale=lean_c[:, t : t + 1])
        w4_dealt = turn([P, N], U32, "w4_dealt", "silu", 3)
        nc.scalar.copy(
            out=w4_dealt[:].rearrange("p (g t m) -> p g t m", g=2, t=PACK),
            in_=w4_raw[:].bitcast(U32).rearrange("p (g m t) -> p g t m", g=2, t=PACK),
        )
        gate = turn([P, PACK, J], F32, "gate", "wide", 2)
        for t in range(PACK):
            for half in range(2):
                look(t, half)

        y = {}
        for half in range(2):
            cols = slice(HALF * half, HALF * (half + 1))
            x_rows = turn([P, PACK, HALF], BF16, "x_rows%d" % half, "rows", 1)
            for t in range(PACK):
                nc.vector.scalar_tensor_tensor(
                    out=x_rows[:, t, :], in0=gate[:, t, cols], scalar=lean_c[:, t : t + 1], in1=leaned[:, t, cols],
                    op0=ALU.mult, op1=ALU.subtract,
                )
            x_bf = turn([P, HALF, PACK], BF16, "x_bf%d" % half, "woven", 2)
            weave(nc.vector.tensor_copy, x_bf, x_rows)
            x_codes = held([P, HALF], U32, "xc%d" % half)
            x_scales = held([P, HALF], U8, "xs%d" % half)
            quantize(x_bf[:].rearrange("p j t -> p (j t)"), x_codes[:], x_scales[:])
            for g in range(2):
                y[g, half] = turn([P, PACK, HALF], F32, "y%d_%d" % (g, half), ("early", "late")[half], 2)
                rows = out_0[512 * g : 512 * (g + 1), cols].rearrange("(p t) j -> p t j", t=PACK)
                for t in range(PACK):
                    wcols = slice(512 * g + BLK * t, 512 * g + BLK * (t + 1))
                    bank = psum.tile([P, HALF], F32, name="y%d_%d_%d" % (g, half, t), tag=("pb", "sb")[g])
                    nc.tensor.matmul_mx(
                        out=bank[:], lhsT=w4_dealt[:, wcols].bitcast(FP8X4), lhsT_scale=w4_sc[:, wcols],
                        rhs=x_codes[:].bitcast(FP8X4), rhs_scale=x_scales[:], start=True, stop=True,
                    )
                    nc.scalar.activation(
                        out=y[g, half][:, t, :], in_=bank[:], func=ACT.Copy, scale=size_c[:, g, t : t + 1]
                    )
                    if t % 2 == 1:
                        nc.sync.dma_start(out=rows[:, t - 1 : t + 1, :], in_=y[g, half][:, t - 1 : t + 1, :])

        y_scales = held([P, 2, J], U8, "y_scales")

        def weave_y(g, half):
            y_bf = turn([P, HALF, PACK], BF16, "y_bf%d_%d" % (g, half), "y_bf", 3)
            weave(nc.vector.tensor_copy, y_bf, y[g, half])
            return y_bf

        def planes_of_y(g, half, y_bf):
            cols = slice(HALF * half, HALF * (half + 1))
            y_codes = held([P, HALF], U32, "yc%d_%d" % (g, half))
            quantize(y_bf[:].rearrange("p j t -> p (j t)"), y_codes[:], y_scales[:, g, cols])
            nc.sync.dma_start(
                out=out_1[g].rearrange("p m t -> p (m t)").bitcast(I32)[:, cols], in_=y_codes[:].bitcast(I32)
            )

        pieces = [(g, half) for half in range(2) for g in range(2)]
        woven = [weave_y(*pieces[0])]
        for i, piece in enumerate(pieces):
            if i + 1 < len(pieces):
                woven.append(weave_y(*pieces[i + 1]))
            planes_of_y(*piece, woven[i])
        for quad in range(4):
            queue = nc.sync if quad % 2 == 0 else nc.scalar
            queue.dma_start(
                out=out_2[:, 4 * quad : 4 * quad + 4, :].rearrange("g r m -> r g m").bitcast(I32),
                in_=y_scales[32 * quad : 32 * quad + 4].bitcast(I32),
            )
